import numpy as np, ml_dtypes
CORES = [35,38,43,46]
N = 4
BF = ml_dtypes.bfloat16
def gentries(a):
    return np.ascontiguousarray(a.reshape(8, 16, -1).transpose(0, 2, 1)).reshape(8, -1)
def gtable(e):
    e = np.asarray(e); return np.ascontiguousarray(e.reshape(8, -1, 16).transpose(0, 2, 1)).reshape(128, -1).astype(np.int32)
W, K, O, TH, CAP, RO = 8192, 8, 256, 200, 32, 5
def ring(rng):
    gap = rng.integers(0, W // K, (N, 8, K, O)) + 1; gap[:, :, 0] = rng.integers(0, W, (N, 8, O))
    return np.add.accumulate(gap, axis=2) & (W - 1)
def held(c, want, pri):
    h = np.zeros(c.shape, np.int64)
    for q in range(N):
        for g in range(8):
            p = np.broadcast_to(pri[q, g], (K, O)); low = np.full(W, O); w = want[q, g]
            np.minimum.at(low, c[q, g][w], p[w]); h[q, g] = w & (low[c[q, g]] == p)
    return h
def crew(rng):
    c = ring(rng); lv = rng.choice(np.array([0, K // 2, K - 2, K - 1, K]), (8, O)); pri = np.zeros((8, O), np.int64); cls = np.zeros((8, 1, O), bool)
    nf = rng.permutation(8 + (O * 45 // 100 - 8) * np.arange(8) // 7)
    for g in range(8):
        n = int(nf[g]); o = rng.permutation(O); lv[g, o[:n]] = K; pri[g, o] = np.arange(O); cls[g, 0, o[:n]] = True
        for q in range(N):
            own = rng.permutation(W)[:n * K].reshape(K, n); c[q, g][:, o[:n]] = own
            rest = c[q, g][:, o[n:]]; t = rng.choice(own.reshape(-1), O - n); k = rng.integers(0, K, O - n)
            ok = (rng.random(O - n) < 0.3) & ~np.any(rest == t, axis=0)
            rest[k[ok], np.flatnonzero(ok)] = t[ok]; c[q, g][:, o[n:]] = rest
    want = (np.arange(K)[:, None] < lv[:, None, :]) & (cls | (rng.random((N, 8, K, O)) < 0.95))
    return c, held(c, want, np.broadcast_to(pri, (N, 8, O)))
def far(rng, m, share, over):
    k = rng.integers(0, K, (N, 8, O)); k = np.where(rng.random(k.shape) < 0.5, k, (K - 1) * rng.integers(0, 2, k.shape))
    hit = (rng.random((N, 8, 1, O)) < share) & (np.arange(K)[:, None] == k[:, :, None, :])
    return np.where(hit, TH + rng.integers(1, over + 1, m.shape), m)
def naps(rng, share):
    return np.add.reduce((rng.random((N, 8, O, RO)) < share).astype(np.int64) << np.arange(RO), axis=3)
def pack(x, c, h, m, wk, lump=None):
    ix = c.reshape(N, 8, 1, K * O); xc = np.take_along_axis(x, ix, 3); m = m.reshape(N, 8, 1, K * O)
    d = (m >> 4) + (((np.arange(16).reshape(16, 1) + ix) & 15) < (m & 15))
    if lump is not None:
        s = lump.reshape(N, 8, 1, K * O); i = (np.arange(16).reshape(16, 1) + s) & 15
        most = np.take_along_axis(np.maximum(xc, 255 - xc), i, 2).astype(np.int64); before = np.add.accumulate(most, axis=2) - most
        u = np.zeros(i.shape, np.int64); np.put_along_axis(u, i, np.minimum(np.maximum(m - before, 0), most), 2)
        d = np.where(s < 16, u, d)
    e = np.where(xc < 128, xc + d, xc - d)
    return {"x": np.ascontiguousarray(x.reshape(N, 128, W)).astype(np.float32).astype(BF), "snap": np.ascontiguousarray(e.reshape(N, 128, K * O)).astype(np.float32).astype(BF),
            "cs": np.stack([gtable(a.reshape(8, -1)) for a in c]), "hold": np.stack([gtable(a.reshape(8, -1)) for a in h]), "wake": np.stack([gtable(a) for a in wk])}
def cells(rng):
    return rng.integers(0, 256, (N, 8, 16, W), dtype=np.int32)
def setup_inputs(rng):
    x = cells(rng); c, h = crew(rng); m = far(rng, rng.integers(0, TH + 1, c.shape), 0.08, 600)
    return pack(x, c, h, m, naps(rng, rng.choice(np.array([0.5, 0.7, 0.9]), (N, 8, 1, 1))))
def setup_inputs_room(rng):
    x = cells(rng); c = np.zeros((N, 8, K, O), np.int64); h = np.ones((N, 8, K, O), np.int64); m = rng.integers(0, TH + 1, c.shape); wk = naps(rng, 0.7)
    cnt = rng.permutation(np.array([0, 1, CAP - 1, CAP, CAP + 1, 2 * CAP, O - 1, O]))
    for g in range(8):
        n = int(cnt[g]); o = rng.permutation(O)
        if n == 0: wk[:, g] = 1
        for q in range(N):
            c[q, g] = rng.permutation(W)[:K * O].reshape(K, O)
            rest = o[n:] if q & 1 else o[n:][rng.random(O - n) < 0.5]
            h[q, g][rng.integers(0, K, len(rest)), rest] = 0
            if q & 1 == 0 and n > 0: m[q, g][rng.integers(0, K), rest[rng.random(len(rest)) < 0.15]] = TH + 1
    return pack(x, c, h, m, wk)
def setup_inputs_storm(rng):
    x = cells(rng); c = ring(rng); m = rng.integers(0, TH + 1, c.shape); want = rng.random(c.shape) < 0.5; wk = naps(rng, 0.8)
    pri = np.argsort(rng.random((N, 8, O)), axis=-1); deal = rng.permutation(8); role = deal & 3
    for g in range(8):
        if deal[g] == 0:
            want[:, g] = True
            for q in range(N): c[q, g] = rng.permutation(W)[:K * O].reshape(K, O)
        if role[g] == 0: m[:, g, rng.integers(0, K)] = TH + 1 + rng.integers(0, 600, (N, O))
        if role[g] == 1: m[::2, g, 0, ::2] = TH + 1
        if role[g] == 2:
            o = int(rng.integers(0, O))
            for q in range(N):
                v = int(rng.integers(0, W)); k = rng.integers(0, K, O); ok = ~np.any(c[q, g] == v, axis=0)
                c[q, g][k[ok], np.flatnonzero(ok)] = v; x[q, g, :, v] = rng.integers(0, 16, 16) + 240 * (q & 1)
                want[q, g, :, o] = True; i = int(np.flatnonzero(pri[q, g] == 0)[0]); pri[q, g, i] = pri[q, g, o]; pri[q, g, o] = 0
        if role[g] == 3: want[:, g] = False; wk[:, g] = wk[:, g] & ~1
    p = 2 * int(rng.integers(0, N // 2)); m[p:p + 2] = far(rng, m, 1.0, 600)[p:p + 2]
    return pack(x, c, held(c, want, pri), m, wk)
def setup_inputs_crowd(rng):
    x = cells(rng); c = np.zeros((N, 8, K, O), np.int64)
    for q in range(N):
        for g in range(8):
            P = 64 if g & 1 else 256
            pool = rng.permutation(np.concatenate([np.array([0, W - 1]), 1 + rng.permutation(W - 2)[:P - 2]]))
            c[q, g] = pool[(rng.integers(0, P, O) + np.arange(K)[:, None] * (2 * rng.integers(0, P // 2, O) + 1)) & (P - 1)]
    pri = np.argsort(rng.random((8, O)), axis=-1); lv = np.where(pri < 3, K, rng.integers(0, K + 1, (8, O)))
    lv[rng.permutation(8)[:4]] = 0
    want = np.broadcast_to(np.arange(K)[:, None] < lv[:, None, :], (N, 8, K, O))
    m = far(rng, rng.integers(0, TH + 1, c.shape), 0.01, 600)
    return pack(x, c, held(c, want, np.broadcast_to(pri, (N, 8, O))), m, naps(rng, rng.choice(np.array([0.6, 1.0]), (N, 8, 1, 1))))
def setup_inputs_ties(rng):
    x = cells(rng); z = rng.random((N, 8, 1, W)); x = np.where(z < 0.06, 0, np.where(z < 0.12, 255, x)).astype(np.int32)
    c, h = crew(rng); m = far(rng, rng.choice(np.array([0, TH - 1, TH]), c.shape), 0.12, 1)
    wk = naps(rng, 0.75) & ~(1 << int(rng.integers(1, 3)))
    return pack(x, c, h, m, wk, np.minimum(rng.integers(0, 32, c.shape), 16))
def setup_inputs_spread(rng):
    x = np.minimum((np.exp2(8.01 * rng.random((N, 8, 1, W))) * rng.random((N, 8, 16, W))).astype(np.int32), 255)
    c, h = crew(rng); m = far(rng, (TH * rng.random(c.shape) ** 4).astype(np.int64), 0.1, 1000)
    share = np.ones((N, 1, 1, 1)) * rng.permutation(np.array([0.0, 0.2, 0.4, 0.6, 0.8, 0.9, 1.0, 1.0])).reshape(1, 8, 1, 1)
    return pack(x, c, h, m, naps(rng, share))
def check_inputs(d):
    bad = []
    for k in ("x", "snap"):
        v = np.asarray(d[k]).astype(np.float32)
        if not (np.all(v >= 0) and np.all(v <= 255) and np.all(v == np.floor(v))): bad.append("range of " + k)
    for k, hi in (("cs", W - 1), ("hold", 1), ("wake", 2 ** RO - 1)):
        if np.min(d[k]) < 0 or np.max(d[k]) > hi: bad.append("range of " + k)
    c = np.stack([gentries(a) for a in d["cs"]]).reshape(N, 8, K, O); h = np.stack([gentries(a) for a in d["hold"]]).reshape(N, 8, K, O)
    s = np.sort(c, axis=2)
    if np.any(s[:, :, 1:] == s[:, :, :-1]): bad.append("cells of an operation differ")
    for q in range(N):
        for g in range(8):
            v = c[q, g][h[q, g] == 1]
            if len(np.unique(v)) != len(v) and "a cell has one holder" not in bad: bad.append("a cell has one holder")
    return bad
def reference(x, snap, cs, hold, wake):
    v = np.zeros((N, 8, 16, W + 1), np.int32)
    v[..., :W] = x.astype(np.float32).astype(np.int32).reshape(N, 8, 16, W)
    e = snap.astype(np.float32).astype(np.int32).reshape(N, 8, 16, K * O)
    c = np.stack([gentries(a) for a in cs]).astype(np.int64).reshape(N, 8, K, O); h = np.stack([gentries(a) for a in hold]).reshape(N, 8, K, O)
    wk = np.stack([gentries(a) for a in wake]).astype(np.int64)
    own = np.arange(O) + 1; lane = np.broadcast_to(np.arange(O), (N, 8, O)); cur = np.array(lane)
    lock = np.zeros((N, 8, W + 1), np.int64)
    np.put_along_axis(lock, np.where(h == 1, c, W).reshape(N, 8, -1), np.broadcast_to(own, c.shape).reshape(N, 8, -1), 2)
    for t in range(RO):
        twin = np.arange(N) ^ (1 + t % (N - 1))
        got = np.take_along_axis(v, c.reshape(N, 8, 1, -1), 3)
        dist = np.add.reduce(np.abs(got - e), axis=2).reshape(N, 8, K, O)
        who = np.take_along_axis(lock, c.reshape(N, 8, -1), 2).reshape(N, 8, K, O); mine = who == own
        bad = np.any(dist > TH, axis=2); full = np.all(mine, axis=2)
        abort = bad | bad[twin]; ready = full & full[twin] & ~abort
        before = np.add.accumulate(ready.astype(np.int64), axis=2) - ready
        commit = ready & (before < CAP); done = abort | commit
        first = np.argmin(mine, axis=2)[:, :, None, :]
        cell = np.take_along_axis(np.take_along_axis(c, first, 2)[:, :, 0], cur, 2); by = np.take_along_axis(np.take_along_axis(who, first, 2)[:, :, 0], cur, 2)
        gone = np.take_along_axis(done, cur, 2); act = (((wk >> t) & 1) == 1) & ~gone & ~np.take_along_axis(full, cur, 2)
        np.put_along_axis(lock, np.where(done[:, :, None, :] & mine, c, W).reshape(N, 8, -1), 0, 2)
        for q in range(N):
            for g in range(8):
                w = np.flatnonzero(act[q, g] & (by[q, g] == 0)); low = np.full(W, O); a = cell[q, g][w]
                np.minimum.at(low, a, w); win = low[a] == w
                lock[q, g][a[win]] = cur[q, g][w[win]] + 1
        cur = np.where(gone, lane, np.where(act & (by > 0), by - 1, cur))
        cm = np.broadcast_to(commit[:, :, None, :], (N, 8, K, O)); dn = np.broadcast_to(done[:, :, None, :], (N, 8, K, O)).reshape(N, 8, 1, -1)
        d = np.where(cm.reshape(N, 8, 1, -1), got[twin], e)
        np.put_along_axis(v, np.where(cm, c, W).reshape(N, 8, 1, -1), d, 3)
        u = np.add.reduce(d.reshape(N, 8, 2, 8, K, O).astype(np.int64), axis=3); hs = (u[:, :, 0] * u[:, :, 1]) >> 3
        new = np.zeros((N, 8, K, O), np.int64); new[:, :, 0] = hs[:, :, 0] & (W - 1)
        for k in range(1, K): new[:, :, k] = (new[:, :, k - 1] + 1 + (hs[:, :, k] & (W // K - 1))) & (W - 1)
        c = np.where(done[:, :, None, :], new, c)
        e = np.where(dn, np.take_along_axis(v, c.reshape(N, 8, 1, -1), 3), e)
    lock[..., W] = 0
    mine = np.take_along_axis(lock, c.reshape(N, 8, -1), 2).reshape(N, 8, K, O) == own
    ys = np.add.reduce(v[..., :W] * np.arange(1, 17, dtype=np.int32).reshape(16, 1), axis=2)
    return {"ys": ys.astype(np.float32), "yc": np.stack([gtable(a.reshape(8, -1)) for a in c]).astype(np.float32),
            "yh": np.stack([gtable(a.reshape(8, -1)) for a in mine]).astype(np.float32), "yl": np.stack([gtable(a) for a in cur]).astype(np.float32)}

from concourse.mybir import AluOpType as OP, ActivationFunctionType as AF

NS = 5
E0, VB, E1 = 0, 2048, 10496
F, B, I, U16 = "float32", "bfloat16", "int32", "uint16"
SCRATCH = {}


def _buf(names, n, d):
    for x in names.split():
        SCRATCH[x] = ("sbuf", [128, n], d)


_buf("VW", 12544, B)
_buf("TT", 10240, F)
_buf("YY", 8448, F)
_buf("ad SEL WR", 2048, B)
_buf("df gt", 1024, B)
_buf("XO EQ", 4096, B)
_buf("SELF WH", 2048, F)
_buf("pI rI gI", 1, I)
_buf("pF rF gF g15 lo8 r1", 1, F)
_buf("uF sG sH ys8 tau tauL cdR clR", 256, F)
_buf("mI mG hI", 128, I)
_buf("ZB ZA ZH", 144, B)
_buf("BO ID IN I8 NI LL TRI LT WY I64", 128, B)
_buf("RM OW J16 JG cur1", 16, F)
_buf("IG CT z256 taub vR dR gR cnR", 256, B)
_buf("JE JE8 JE9 AGs oc oh fc", 128, F)
_buf("WHT", 1024, F)
_buf("thR", 264, F)
_buf("ST", 1280, B)
_buf("aw", 80, F)
_buf("awI", 80, I)
_buf("z32", 32, B)
_buf("OWb", 16, B)
_buf("wI", 16, I)
_buf("clU", 256, U16)
_buf("GG", 512, B)
_buf("tw", 2200, F)
_buf("tx", 3400, F)
_buf("ti", 3000, I)
_buf("tb", 2400, B)
_buf("tu", 1400, U16)
_buf("FL FR", 32 * NS, B)
_buf("NG NR", 128 * NS, I)
_buf("CO CR", 256 * NS, B)
for _n in ("D1", "D2", "PA", "X1", "MK", "M1", "M2", "M3"):
    SCRATCH["ps" + _n] = ("psum", [128, 512], F)
LOADS = ["dcs", "dho", "dwk", "dsn", "dx"]
SEMAPHORES = ["sv", "ss", "st", "sg", "lsem", "oc_", "oh_", "ol_", "oy_"] + LOADS + [k + str(t) for k in "fnc" for t in range(NS)]
CY = 0.00083 * 1.15


def rank_program(g, core, T, topo):
    rank = T.rank_of(core)
    if rank is None:
        return
    eng = {"v": g.vector, "s": g.scalar, "t": g.tensor, "g": g, "y": g.sync}
    esem = {"v": "sv", "s": "ss", "t": "st", "g": "sg"}
    ops = []

    def A(name, a=0, b=None, step=1):
        b = SCRATCH[name][1][1] if b is None else b
        return ((T[name][:, a:b] if step == 1 else T[name][:, a:b:step]), ((name, a, b),), (b - a + step - 1) // step,
                SCRATCH[name][2] in (B, U16), "ps" if name[:2] == "ps" else "sb")

    def IND(w, off):
        wn, a, b = w
        on, c, d = off[1][0]
        return T[wn][:, a:b].indirect(off[0]), ((wn, a, b), (on, c, d)), 16 * (d - c), SCRATCH[wn][2] == B, "ind"

    def part(o, a, b):
        name, s, _e = o[1][0]
        return A(name, s + a, s + b)

    def op(e, call, outs, ins, cost, sem=None, inc=1, arr=None):
        rd = [x for o in ins for x in o[1]]
        wr = []
        for o in outs:
            wr.append(o[1][0])
            rd += list(o[1][1:])
        ops.append({"e": e, "call": call, "rd": rd, "wr": wr, "cost": cost, "sem": sem or esem.get(e), "inc": inc, "arr": arr, "mm": None})

    def vcost(o, ins, n, two=False):
        if o[4] == "ind":
            return 0.05 + n * 3.0 * CY
        if any(x[4] == "ind" for x in ins):
            return 0.05 + n * 1.5 * CY
        return max(64, n * (2 if two and all(x[4] == "sb" for x in ins) else 0.5 if not two and o[3] and ins[0][3] else 1)) * CY

    def tt(o, a, b, f):
        op("v", lambda: g.vector.tensor_tensor(o[0], a[0], b[0], f), [o], [a, b], vcost(o, [a, b], b[2], True))

    def ts(o, a, s1, f1, s2=None, f2=None):
        col = [s1] if isinstance(s1, tuple) else []
        x1 = s1[0] if col else s1
        if f2 is None:
            op("v", lambda: g.vector.tensor_scalar(o[0], a[0], x1, None, f1), [o], [a] + col, vcost(o, [a], a[2]))
        else:
            op("v", lambda: g.vector.tensor_scalar(o[0], a[0], x1, s2, f1, f2), [o], [a] + col, vcost(o, [a], a[2]))

    def cp(o, a):
        op("v", lambda: g.vector.tensor_copy(o[0], a[0]), [o], [a], vcost(o, [a], a[2]))

    def ms(o, v):
        op("v", lambda: g.vector.memset(o[0], v), [o], [], max(64, o[2] * (0.5 if o[3] else 1)) * CY)

    def act(o, a, func=AF.Copy, bias=0.0, scale=1.0):
        c = 0.065 + a[2] * (3.0 if o[4] == "ind" else 1.5) * CY if "ind" in (o[4], a[4]) else max(64, a[2]) * CY
        col = [scale] if isinstance(scale, tuple) else []
        x = scale[0] if col else scale
        if not col and bias == 0.0 and scale == 1.0:
            op("s", lambda: g.scalar.activation(o[0], a[0], func), [o], [a], c)
        else:
            op("s", lambda: g.scalar.activation(o[0], a[0], func, bias=bias, scale=x), [o], [a] + col, c)

    def mm(lst, first=True, last=True):
        c = sum(max(64, x[2][2]) * (1 if x[1][3] else 4) for x in lst) * 0.00042 * 1.15
        op("t", None, [x[0] for x in lst], [y for x in lst for y in x[1:]], c)
        ops[-1]["mm"] = (lst, first, last)

    def win(z, i):
        return A(z, 15 - i, 143 - i)

    def to_w(o, src, sel="SEL"):
        n = 2 if sel == "SELF" else 16
        for j in range(0, 16, n):
            mm([(o, A(sel, 128 * i, 128 * i + 128), A(src, i, 256, 16)) for i in range(j, j + n)], j == 0, j + n == 16)

    def to_r(on, a, srcs):
        lst = []
        for i in range(16):
            lst.append([(A(on, a + i, a + 256, 16), A("WR", 128 * i, 128 * i + 128), s) for s in srcs])
        op("t", None, [A(on, a, a + 256)], [A("WR")] + srcs, 16 * len(srcs) * 64 * 0.00042 * 1.15)
        ops[-1]["mm"] = (lst, True, True)

    def rep(on, a, src):
        op("t", None, [A(on, a, a + 128)], [A("ID"), src], 8 * 64 * 0.00042 * 1.15)
        ops[-1]["mm"] = ([[(A(on, a + 16 * k, a + 16 * k + 16), A("ID"), src)] for k in range(8)], True, True)

    def load(e, sem, o, tin):
        op(e, lambda: eng[e].dma_start(o[0], tin), [o], [], 0.1, sem, 16, 2.5 + o[2] * (2 if o[3] else 4) * 128 / 200e3)
        ops[-1]["load"] = True

    twins = [T.cores[rank ^ (1 + t % 3)] for t in range(NS)]
    narr = [len(topo.engines(d, core)[:8]) for d in twins]
    nsent = [0]

    def send(t, sb, rb, w, key):
        dst = twins[t]
        rid, pid, _se = topo.addr(dst)
        es = topo.engines(core, dst)[:8]
        s, r = A(sb, w * t, w * t + w), A(rb, w * t, w * t + w)
        op("g", lambda: g.remote_dma(out_ap=r[0], in_ap=s[0], remote_sem=T.sem[key + str(t)], local_sem=T.sem.lsem, pid=pid, routing_id=rid,
                                     dma_engine_mask=sum(1 << x for x in es)), [], [s], 0.8, "lsem", len(es))
        op("a", None, [(None, ((rb, w * t, w * t + w),))], [s], 0.0, key + str(t), narr[t], 2.0 + w / 256.0)
        ops[-1]["send"] = len(ops) - 2
        nsent[0] += len(es)

    tops = {"tw": 0, "tx": 0, "ti": 0, "tb": 0, "tu": 0}

    def new(k, n):
        a = tops[k]
        if a + n > SCRATCH[k][1][1]:
            a = 0
        tops[k] = a + (n + 15) // 16 * 16
        return A(k, a, a + n)

    cI, cU = new("ti", 128), new("tu", 128)
    load("s", "dcs", cI, T.cs[:])
    load("s", "dho", A("hI"), T.hold[:])
    load("y", "dsn", A("VW", E0, E0 + 2048), T.snap[:])
    load("y", "dx", A("VW", VB, VB + 8192), T.x[:])
    load("s", "dwk", A("wI"), T.wake[:])

    def iota(o, pattern, base, cm, flag=True):
        c = 0.13 + 2 * o[2] * CY
        if flag:
            op("g", lambda: g.iota(o[0], pattern, base, cm, allow_small_or_imprecise_dtypes=True), [o], [], c)
        else:
            op("g", lambda: g.iota(o[0], pattern, base, cm), [o], [], c)
    iota(A("pI"), [[1, 1]], 0, 1, False)
    iota(A("uF"), [[1, 256]], 0, 0)
    iota(A("mI"), [[1, 128]], 0, 0, False)
    iota(A("JE"), [[16, 128]], 0, 0)
    iota(A("sG"), [[16, 2], [0, 8], [1, 16]], 936, 0)
    iota(A("WH"), [[0, 8], [1, 256]], 33, 0)
    ms(A("TT", 0, 4096), 0.0)
    ts(A("rI"), A("pI"), 15, OP.bitwise_and)
    ts(A("gI"), A("pI"), 112, OP.bitwise_and)
    ts(A("mG"), A("mI"), 112, OP.bitwise_and)
    cp(A("pF"), A("pI"))
    cp(A("rF"), A("rI"))
    cp(A("gF"), A("gI"))
    ts(A("g15"), A("gF"), 15.0, OP.add)
    ts(A("lo8"), A("rF"), 8.0, OP.is_lt)
    ts(A("r1"), A("rF"), 1.0, OP.add)
    ts(A("JE"), A("JE"), A("rF"), OP.add)
    cp(A("OW"), A("JE", 0, 16))
    ts(A("OWb"), A("OW"), 1.0, OP.add)
    ts(A("J16"), A("JE", 0, 16), 8192.0, OP.add)
    ts(A("JE8"), A("JE"), 8192.0, OP.add)
    ts(A("JE9"), A("JE"), 8448.0, OP.add)
    for q in range(4):
        act(A("TT", 4096 + 1024 * q, 5120 + 1024 * q), A("TT", 1024 * q, 1024 * q + 1024))
    x1, x2, x3, tl = new("tx", 128), new("tx", 128), new("tx", 128), new("tu", 128)
    tt(x1, cI, A("JE8"), OP.subtract)
    tt(x2, x1, A("hI"), OP.mult)
    tt(x3, x2, A("JE8"), OP.add)
    cp(tl, x3)
    act(IND(("TT", 0, 10240), tl), A("WH"), AF.Silu)
    cp(cU, cI)
    Uh = new("tb", 128)
    ts(Uh, A("hI"), -1.0, OP.mult, 1.0, OP.add)
    ts(A("ZB"), A("uF", 0, 144), A("g15"), OP.is_equal)
    ts(A("ZA"), A("ZB"), A("lo8"), OP.mult)
    tt(A("ZH"), A("ZB"), A("ZA"), OP.subtract)
    ts(A("BO"), A("mG"), A("gF"), OP.is_equal)
    op("g", lambda: g.affine_select(T.LL[:], T.BO[:], [[-1, 128]], OP.is_ge, 0.0, 0, 1), [A("LL")], [A("BO")], 0.4)
    ts(A("ID"), A("uF", 0, 128), A("pF"), OP.is_equal)
    ts(A("I8"), A("ID"), 8.0, OP.mult)
    ts(A("IN"), A("ID"), -1.0, OP.mult)
    ts(A("NI"), A("ID"), -4096.0, OP.mult)
    ts(A("RM"), A("uF", 0, 16), A("rF"), OP.is_equal)
    ts(A("WY"), A("BO"), A("r1"), OP.mult)
    for i in range(16):
        ts(A("WR", 128 * i, 128 * i + 128), A("BO"), A("RM", i, i + 1), OP.mult)
        ts(A("SEL", 128 * i, 128 * i + 128), A("ID"), A("RM", i, i + 1), OP.mult)
        act(A("SELF", 128 * i, 128 * i + 128), A("ID"), AF.Copy, 0.0, A("RM", i, i + 1))
    ts(A("I64"), A("ID"), -64.0, OP.mult)
    tt(A("TRI"), A("I64"), A("LL"), OP.subtract)
    tt(A("LT"), A("BO"), A("LL"), OP.subtract)
    for h in range(2):
        tt(A("sH", 128 * h, 128 * h + 128), A("sG", 128 * h, 128 * h + 128), A("BO"), OP.mult)
    ts(A("IG"), A("sH"), -1000.0, OP.add)
    ts(A("JG"), A("OW"), 256.0, OP.add)
    ms(A("thR"), 1000000.0)
    thW = new("tb", 16)
    ms(thW, 0.0)
    ts(A("thR", 1, 257), A("uF"), 33.0 - 1.0 / 128, OP.add)
    ms(A("z32"), 0.0)
    ms(A("z256"), 0.0)
    ms(A("VW", VB + 8192, VB + 8448), 0.0)
    ms(A("GG"), 0.0)
    for t in range(NS):
        ms(A("ST", 256 * t, 256 * t + 256), float(t + 1))
        ts(A("awI", 16 * t, 16 * t + 16), A("wI"), t, OP.arith_shift_right, 1, OP.bitwise_and)
        if t < NS - 1:
            ts(A("WHT", 256 * t, 256 * t + 256), A("WH", 0, 256), (t + 1) / 64.0, OP.add)
    cp(A("aw"), A("awI"))
    cur, curU, cur1 = A("OW"), new("tu", 16), A("cur1")
    cp(curU, A("OW"))
    ts(cur1, A("OW"), 1.0, OP.add)

    def sums(src, a, n, c, last=False):
        for z, p in (("ZA", 0), ("ZH", 128)):
            mm([(A("psPA", p + c, p + c + n // 16), win(z, i), A(src, a + i, a + n, 16)) for i in range(16)], False, last and p > 0)

    def zero():
        mm([(A("psPA", 0, 256), A("ID"), A("z256"))], True, False)

    def hashes(o):
        act(A("AGs"), A("psPA", 0, 128))
        pr, hh = new("ti", 128), new("ti", 128)
        tt(pr, A("psPA", 128, 256), A("AGs"), OP.mult)
        ts(part(hh, 0, 16), part(pr, 0, 16), 3, OP.arith_shift_right, 8191, OP.bitwise_and)
        ts(part(hh, 16, 128), part(pr, 16, 128), 3, OP.arith_shift_right, 1023, OP.bitwise_and)
        ts(part(hh, 16, 128), part(hh, 16, 128), 1.0, OP.add)
        for k in range(1, 8):
            tt(part(hh, 16 * k, 16 * k + 16), part(hh, 16 * k, 16 * k + 16), part(hh, 16 * k - 16, 16 * k), OP.add)
        ts(o, hh, 8191, OP.bitwise_and)

    def split_cells():
        lo, x = new("ti", 128), new("tx", 128)
        ts(lo, cI, 63, OP.bitwise_and)
        tt(x, cI, lo, OP.subtract)
        cp(A("CT", 128, 256), lo)
        act(A("CT", 0, 128), x, AF.Copy, -16384.0)

    def claimed(t):
        x = new("tx", 128)
        o = new("tb", 128)
        ts(st["cl"], A("psM2", 80, 96), float(t + 1), OP.is_equal)
        rep("psM3", 256, st["cl"])
        tt(x, A("psM3", 256, 384), st["fm"], OP.mult)
        tt(o, st["U1"], x, OP.subtract)
        return o

    def lock(t):
        x, y, z, l = new("tw", 16), new("tw", 16), new("tw", 16), new("tu", 16)
        tt(x, st["cf"], A("J16"), OP.subtract)
        tt(y, x, st["cl"], OP.mult)
        tt(z, y, A("J16"), OP.add)
        cp(l, z)
        act(IND(("TT", 0, 10240), l), A("WHT", 256 * t, 256 * t + 256), AF.Silu)

    st = {}
    zero()
    sums("VW", E0, 2048, 0, True)
    NE = new("ti", 128)
    hashes(NE)
    split_cells()
    dec = None

    for t in range(NS):
        eb = (E0, E0, E1, E0, E1)[t]
        lastt = t == NS - 1
        zero()
        sums("VW", eb, 1024, 0)
        if t > 0:
            Uh = claimed(t - 1)
        for p in range(2):
            j = 512 * p
            tt(A("df", j, j + 512), IND(("VW", VB, VB + 8192), part(cU, 32 * p, 32 * p + 32)), A("VW", eb + j, eb + j + 512), OP.subtract)
            act(A("gt", j, j + 512), IND(("VW", VB, VB + 8192), part(cU, 64 + 32 * p, 96 + 32 * p)))
            x = ("psX1", "psD2")[p]
            mm([(A(x), A("IN"), A("VW", eb + 1024 + j, eb + 1536 + j))], True, False)
            mm([(A(x), A("ID"), A("gt", j, j + 512))], False, True)
        for p in range(2):
            act(A("ad", 512 * p, 512 * p + 512), A("df", 512 * p, 512 * p + 512), AF.Abs)
        mm([(A("psD1", 0, 64), win("ZB", i), A("ad", i, 1024, 16)) for i in range(16)], True, t == 0)
        if t > 0:
            mm([(A("psD1", 16 * k, 16 * k + 16), A("NI"), dec) for k in range(4)], False, True)
        b1 = new("tx", 64)
        act(b1, A("psD1", 0, 64))
        for p in range(2):
            act(A("ad", 1024 + 512 * p, 1536 + 512 * p), A(("psX1", "psD2")[p]), AF.Abs)
        mm([(A("psM2", 128, 192), win("ZB", i), A("ad", 1024 + i, 2048, 16)) for i in range(16)], True, t == 0)
        if t > 0:
            mm([(A("psM2", 128 + 16 * k, 144 + 16 * k), A("NI"), dec) for k in range(4)], False, True)
        mm([(A("psM3", 16 * s, 128), A("ID" if s == 0 else "I8"), part(Uh, 0, 128 - 16 * s)) for s in range(8)])
        mm([(A("psM3", 128, 144), A("ID"), part(Uh, 16 * k, 16 * k + 16)) for k in range(8)])
        Ft, nf, fm = new("tw", 16), new("tw", 16), new("tb", 128)
        act(Ft, A("psM3", 128, 144), AF.Copy, 200.5, -30000.0)
        act(nf, A("psM3", 128, 144), AF.Sign)
        ts(fm, A("psM3", 0, 128), 1.0, OP.is_equal)
        m1, m2, m3 = new("tx", 64), new("tx", 32), new("tw", 16)
        tt(m1, A("psM2", 128, 192), b1, OP.max)
        tt(m2, part(m1, 0, 32), part(m1, 32, 64), OP.max)
        tt(m3, part(m2, 0, 16), part(m2, 16, 32), OP.max)
        f = 32 * t
        tt(A("FL", f, f + 16), Ft, m3, OP.is_gt)
        ts(A("FL", f + 16, f + 32), m3, 200.0, OP.is_gt)
        send(t, "FL", "FR", 32, "f")
        sums("df", 0, 1024, 0)
        sums("gt", 0, 1024, 64, True)
        NG = A("NG", 128 * t, 128 * t + 128)
        hashes(NG)
        send(t, "NG", "NR", 128, "n")
        if lastt:
            for q in range(16):
                b = ("psX1", "psPA")[q & 1]
                mm([(A(b), A("WY"), A("VW", VB + 512 * q, VB + 512 * q + 512))])
                (act if q % 8 < 5 else cp)(A("YY", 512 * q, 512 * q + 512), A(b))
        if t > 0:
            lock(t - 1)
        cf, cfU, who = new("tw", 16), new("tu", 16), new("tu", 16)
        fc = A("fc")
        tt(fc, fm, cI, OP.mult)
        tt(part(fc, 0, 64), part(fc, 0, 64), part(fc, 64, 128), OP.add)
        tt(part(fc, 0, 32), part(fc, 0, 32), part(fc, 32, 64), OP.add)
        tt(cf, part(fc, 0, 16), part(fc, 16, 32), OP.add)
        cp(cfU, cf)
        act(A("tau"), IND(("TT", 0, 8192), cfU))
        act(A("taub"), IND(("tau", 0, 256), curU), AF.Copy, -32.0)
        act(A("tauL"), IND(("tau", 0, 256), curU))
        to_w(A("psM2", 96, 112), "taub")
        cp(who, A("psM2", 96, 112))
        tt(A("vR"), IND(("thR", 0, 264), who), A("tauL"), OP.is_le)
        to_w(A("psM2", 112, 128), "vR")
        cf1, k1, k2, kb = new("tw", 16), new("ti", 16), new("ti", 16), new("tb", 32)
        act(cf1, cf, AF.Copy, 1.0)
        tt(k1, cf1, nf, OP.mult)
        ts(k2, k1, 127, OP.bitwise_and)
        cp(part(kb, 16, 32), k2)
        tt(part(kb, 0, 16), k1, k2, OP.subtract)
        to_r("psM1", 256, [part(kb, 0, 16), part(kb, 16, 32)])
        act(A("cdR"), A("psM1", 256, 512))
        act(A("clR"), IND(("cdR", 0, 256), curU))
        to_w(A("psM3", 160, 176), "clR", "SELF")
        ts(A("clU"), A("clR"), 0.0, OP.add)
        if t > 0:
            x1, x2, o = new("tx", 128), new("tx", 128), new("ti", 128)
            tt(x1, A("psMK", 384, 512), NG, OP.mult)
            tt(x2, A("psMK", 256, 384), NE, OP.mult)
            tt(o, x1, x2, OP.add)
            NE = o
            if not lastt:
                x3, x4, x5, EL = new("tx", 128), new("tx", 128), new("tx", 128), new("tu", 128)
                ts(x3, cI, 2048.0 if eb == E0 else -16384.0, OP.add)
                tt(x4, A("psMK", 384, 512), x3, OP.mult)
                if eb == E0:
                    tt(x5, x4, A("JE"), OP.max)
                else:
                    ts(x3, x4, 16384.0, OP.add)
                    tt(x5, x3, A("JE9"), OP.min)
                cp(EL, x5)
                for p in range(4):
                    o, w0, w1 = (E1, E0, VB + 8192) if eb == E0 else (E0, VB, E1 + 2048)
                    act(A("VW", o + 512 * p, o + 512 * p + 512), IND(("VW", w0, w1), part(EL, 32 * p, 32 * p + 32)))
        aw = A("aw", 16 * t, 16 * t + 16)
        lc = A("psM3", 160, 176)
        w = [new("tw", 16) for _ in range(10)]
        want, stay, home, back = w[2], w[7], w[8], w[9]
        tt(w[0], A("psM2", 112, 128), aw, OP.mult)
        tt(w[1], aw, w[0], OP.subtract)
        tt(want, lc, w[1], OP.mult)
        act(w[3], lc, AF.Sign)
        tt(w[4], w[0], w[3], OP.mult)
        cp(w[5], who)
        tt(w[6], w[5], cur1, OP.subtract)
        tt(w[6], w[6], w[4], OP.mult)
        tt(stay, w[6], cur, OP.add)
        tt(home, A("OW"), stay, OP.subtract)
        tt(back, cur, A("JG"), OP.subtract)
        rdy, cum, ab, cm, dec, keep = [new("tb", 16) for _ in range(6)]
        tt(rdy, A("FL", f, f + 16), A("FR", f, f + 16), OP.mult)
        (lambda c, r: op("v", lambda: g.vector.tensor_tensor_scan(c[0], r[0], T.z32[:, 0:16], 0.0, OP.add, OP.add), [c], [r, A("z32")], 64 * CY))(cum, rdy)
        tt(ab, A("FL", f + 16, f + 32), A("FR", f + 16, f + 32), OP.max)
        mm([(A("psD2", 64, 80), A("TRI"), rdy), (A("psD2", 64, 80), A("BO"), cum)])
        ts(cm, A("psD2", 64, 80), -32.0, OP.is_lt)
        tt(dec, ab, cm, OP.max)
        mm([(A("psD1", 128, 160), A("ID"), A("z32"))], True, False)
        for c in range(16):
            ts(A("XO", 256 * c, 256 * c + 256), A("IG"), A("psD2", 64 + c, 65 + c), OP.is_equal)
            mm([(A("psD1", 128 + h, 160, 2), A("XO", 256 * c + 128 * h, 256 * c + 128 * h + 128), A("CT", c, 256, 16)) for h in range(2)], False, c == 15)
        z1, z2, z3, zU = new("tw", 16), new("tw", 16), new("tw", 16), new("tu", 16)
        act(z1, A("psD1", 144, 160), AF.Copy, 16384.0)
        tt(z2, A("psD1", 128, 144), z1, OP.add)
        tt(z3, z2, A("J16"), OP.min)
        cp(zU, z3)
        cp(A("CO", 256 * t, 256 * t + 256), IND(("VW", VB, VB + 8448), zU))
        send(t, "CO", "CR", 256, "c")
        act(keep, dec, AF.Copy, 1.0, -1.0)
        for q, s in enumerate((ab, cm, keep, dec)):
            rep("psMK", 128 * q, s)
        x1, x2, x3, x4, o, ou, u1 = [new("tx", 128) for _ in range(4)] + [new("ti", 128), new("tu", 128), new("tb", 128)]
        tt(x1, A("psMK", 0, 128), NE, OP.mult)
        tt(x2, A("psMK", 128, 256), A("NR", 128 * t, 128 * t + 128), OP.mult)
        tt(x3, x1, x2, OP.max)
        tt(x4, A("psMK", 256, 384), cI, OP.mult)
        tt(o, x3, x4, OP.max)
        cI = o
        if not lastt:
            cU = ou
            cp(cU, cI)
            split_cells()
        tt(u1, A("psMK", 384, 512), Uh, OP.max)
        to_r("psM1", 0, [dec])
        act(A("dR"), A("psM1", 0, 256))
        act(A("gR"), IND(("dR", 0, 256), curU))
        gone = A("psM2", 32, 48)
        to_w(gone, "gR")
        al, ca, wn, hm, nc, ncu = [new("tw", 16) for _ in range(5)] + [new("tu", 16)]
        act(al, gone, AF.Copy, 1.0, -1.0)
        tt(ca, want, al, OP.mult)
        act(wn, ca, AF.Sign)
        tt(hm, gone, home, OP.mult)
        tt(nc, hm, stay, OP.add)
        cur, curU, cur1 = nc, ncu, new("tw", 16)
        cp(curU, cur)
        act(cur1, cur, AF.Copy, 1.0)
        for c in range(16):
            ts(A("EQ", 272 * c, 256 * c + 256), A("clU", 16 * c, 256), part(ca, c, c + 1), OP.is_equal)
        mm([(A("psM1", 0, 256), A("LT"), A("EQ", 0, 256)), (A("psM1", 16, 256), A("LL"), A("EQ", 16, 256))], True, False)
        for c in range(1, 16):
            l = [(A("psM1", 16 * c + 16, 256), A("BO"), A("EQ", 272 * c + 16, 256 * c + 256))] if c < 15 else []
            mm(l + [(A("psM1", 16 * c, 16 * c + 16), A("LT"), A("EQ", 272 * c, 272 * c + 16))], False, c == 15)
        act(A("cnR"), A("psM1", 0, 256))
        to_w(A("psM2", 64, 80), "cnR")
        w = [new("tw", 16) for _ in range(4)]
        gU = new("tu", 16)
        ts(w[0], A("psM2", 64, 80), 0.0, OP.is_equal)
        tt(w[1], w[0], wn, OP.mult)
        tt(w[2], w[1], back, OP.mult)
        tt(w[3], w[2], A("JG"), OP.add)
        cp(gU, w[3])
        cp(IND(("GG", 0, 512), gU), A("ST", 256 * t, 256 * t + 256))
        to_w(A("psM2", 80, 96), "GG")
        st = {"cl": new("tb", 16), "cf": cf, "fm": fm, "U1": u1}
        if lastt:
            mm([(A("psD1", 0, 256), A("WY"), A("CR", 256 * t, 256 * t + 256))])
            act(A("ys8"), A("psD1", 0, 256))
            cp(A("oc"), cI)
            ts(A("oh"), claimed(t), -1.0, OP.mult, 1.0, OP.add)
            cp(IND(("YY", 0, 8448), zU), A("ys8"))
        else:
            cp(IND(("VW", VB, VB + 8448), zU), A("CR", 256 * t, 256 * t + 256))
            x, y = new("tw", 16), new("tb", 16)
            act(x, dec, AF.Copy, 0.0, (t + 2) / 64.0)
            tt(y, thW, x, OP.max)
            thW = y
            to_r("psM1", 256, [A("OWb"), thW])
            act(A("thR", 1, 257), A("psM1", 256, 512), AF.Copy, 32.0 - 1.0 / 128)
    for sem, tout, o in (("oc_", T.yc[:], A("oc")), ("ol_", T.yl[:], cur), ("oh_", T.yh[:], A("oh"))):
        (lambda sem, tout, o: op("y", lambda: g.sync.dma_start(tout, o[0]), [], [o], 0.1, sem, 16, 2.5))(sem, tout, o)
    yo = (T.YY[0:128:16, 0:8192], (("YY", 0, 8192),), 8192, False, "sb")
    op("y", lambda: g.sync.dma_start(T.ys[:], yo[0]), [], [yo], 0.1, "oy_", 16, 2.5)

    n = len(ops)
    deps = [set() for _ in range(n)]
    log = {}
    for i, o in enumerate(ops):
        for w, acc in ((False, o["rd"]), (True, o["wr"])):
            for name, a, b in acc:
                ps = name[:2] == "ps"
                for a2, b2, w2, k in log.get(name, []):
                    if k != i and ((ps and (ops[k]["e"] != o["e"] or o["e"] == "t")) or (a < b2 and a2 < b and (w or w2))):
                        deps[i].add(k)
        for w, acc in ((False, o["rd"]), (True, o["wr"])):
            for name, a, b in acc:
                old = log.get(name, [])
                if w:
                    old = [r for r in old if not (a <= r[0] and r[1] <= b)]
                log[name] = old + [(a, b, w, i)]
        if "send" in o:
            deps[i].add(o["send"])
    succ = [[] for _ in range(n)]
    for i in range(n):
        for k in deps[i]:
            succ[k].append(i)
    lat = [(o["arr"] if o["arr"] is not None else 0.13) for o in ops]
    prio = [0.0] * n
    for i in range(n - 1, -1, -1):
        prio[i] = ops[i]["cost"] + max([lat[i] + prio[k] if ops[k]["e"] != ops[i]["e"] or ops[i]["e"] != "t" else prio[k] for k in succ[i]] + [0.0])
    for i in range(n):
        if "load" in ops[i]:
            prio[i] = 1e6 - i
    left = [len(d) for d in deps]
    ready = {}
    rt = [0.0] * n
    for i in range(n):
        if not left[i]:
            ready.setdefault(ops[i]["e"], []).append(i)
    free = {e: 0.0 for e in "vstgya"}
    order = []
    while len(order) < n:
        best = None
        for e, l in ready.items():
            if not l:
                continue
            t0 = max(free[e], min(rt[i] for i in l))
            if best is None or t0 < best[0]:
                best = (t0, e)
        t0, e = best
        i = max([i for i in ready[e] if rt[i] <= t0 + 1e-9], key=lambda i: (prio[i], -i))
        ready[e].remove(i)
        order.append(i)
        if e != "a":
            free[e] = t0 + ops[i]["cost"]
        for k in succ[i]:
            d = 0.0 if ops[i]["e"] == ops[k]["e"] == "t" else 0.0 if ops[i]["e"] == "g" and ops[k]["e"] == "a" else lat[i]
            rt[k] = max(rt[k], t0 + ops[i]["cost"] + d)
            left[k] -= 1
            if not left[k]:
                ready.setdefault(ops[k]["e"], []).append(k)

    cnt = {}
    known = {e: {} for e in "vstgya"}
    clocks = {}
    log = {}

    def waits(e, acc, w):
        own = esem.get(e)
        for name, a, b in acc:
            ps = name[:2] == "ps"
            for a2, b2, w2, sem, m in log.get(name, []):
                ov = a < b2 and a2 < b
                if (ov and w2 and (e != "t" or not w)) if sem == own else (ps or (ov and (w or w2))):
                    if known[e].get(sem, 0) < m:
                        eng[e].wait_ge(T.sem[sem], m)
                        for q, v in list(clocks[(sem, m)].items()):
                            known[e][q] = max(known[e].get(q, 0), v)

    def note(sem, m, acc, w):
        for name, a, b in acc:
            ps = name[:2] == "ps"
            log[name] = [r for r in log.get(name, []) if not ((w and a <= r[0] and r[1] <= b) or (ps and r[3] != sem)
                                                              or (r[3] == sem and r[2] == w and a <= r[0] and r[1] <= b))] + [(a, b, w, sem, m)]

    for i in order:
        o = ops[i]
        e, sem = o["e"], o["sem"]
        m = cnt[sem] = cnt.get(sem, 0) + o["inc"]
        if e == "a":
            clocks[(sem, m)] = {sem: m}
            note(sem, m, o["wr"], True)
            continue
        if o["mm"] is None:
            waits(e, o["rd"], False)
            waits(e, o["wr"], True)
            x = o["call"]()
            if sem != "lsem":
                x.then_inc(T.sem[sem], o["inc"])
        else:
            lst, first, last = o["mm"]
            runs = lst if isinstance(lst[0], list) else [lst]
            for run in runs:
                for q, (po, pl, pr) in enumerate(run):
                    waits(e, pl[1] + pr[1], False)
                    waits(e, po[1], True)
                    x = g.tensor.matmul(po[0], pl[0], pr[0], first and q == 0, last and q == len(run) - 1)
            x.then_inc(T.sem.st, 1)
        if sem == "lsem":
            continue
        clocks[(sem, m)] = dict(known[e])
        clocks[(sem, m)][sem] = m
        note(sem, m, o["rd"], False)
        note(sem, m, o["wr"], True)
    for s in ("oc_", "ol_", "oh_", "oy_"):
        g.sync.wait_ge(T.sem[s], 16)
    g.wait_ge(T.sem.lsem, nsent[0])
    for s in ("sv", "ss", "st", "sg"):
        g.wait_ge(T.sem[s], cnt[s])
